import numpy as np
import ml_dtypes


def mxq(x, axis, fmt="e4m3"):
    dtype, down = {"e4m3": (ml_dtypes.float8_e4m3fn, 7), "e5m2": (ml_dtypes.float8_e5m2, 14)}[fmt]
    v = np.moveaxis(np.asarray(x, np.float32).astype(ml_dtypes.bfloat16).astype(np.float64), axis, -1)
    blocks = v.reshape(v.shape[:-1] + (-1, 32))
    amax = np.abs(blocks).max(-1, keepdims=True)
    byte = np.maximum(np.where(amax > 0, np.frexp(amax)[1] - 1 + 127, 0) - down, 1)
    scale = np.exp2(byte - 127.0)
    codes = (blocks / scale).astype(np.float32).astype(dtype).astype(np.float64)
    return np.moveaxis((codes * scale).reshape(v.shape), -1, axis)


WIDE = False


def mx_kscale(k):
    if not WIDE:
        return np.ones(k)
    levels = np.array([10, -10, 5, -5, 0])
    if k % 512:
        return np.exp2(np.random.permutation(np.resize(levels, k // 32))).repeat(32)
    a = np.empty((k // 512, 16))
    for p in range(k // 512):
        a[p, :8] = np.random.permutation(np.resize(levels, 8))
        for g in range(8):
            far = levels[np.abs(levels - a[p, g]) >= 10]
            a[p, g + 8] = far[np.random.randint(len(far))]
    return np.exp2(a.ravel()).repeat(32)


def f64(x):
    return np.asarray(x).astype(np.float64)


def striped(idx):
    return np.tile(idx.reshape(-1, 16).T, (8, 1)).astype(np.uint16)


def unstriped(offs):
    return offs[:16].T.reshape(-1).astype(np.int64)


def pack_weight(w):
    k, n = w.shape
    w = f64(np.asarray(w, np.float32).astype(ml_dtypes.bfloat16)).reshape(k // 32, 32, n)
    amax = np.abs(w).max(1)
    byte = np.clip(np.where(amax > 0, np.frexp(amax)[1] - 1 + 127 - 7, 1), 1, 254)
    scaled = (w * np.exp2(127.0 - byte)[:, None, :]).reshape(k, n).astype(np.float32)
    words = np.ascontiguousarray(scaled.reshape(k // 512, 128, 4, n).transpose(0, 1, 3, 2)).astype(ml_dtypes.float8_e4m3fn).view(np.uint8)
    return words, np.ascontiguousarray(byte.astype(np.uint8).reshape(k // 512, 16, n))


def unpack_weight(words, scales):
    g, p, n, _ = words.shape
    vals = np.ascontiguousarray(words).view(ml_dtypes.float8_e4m3fn).astype(np.float64) * np.repeat(np.exp2(scales.astype(np.float64) - 127.0), 8, axis=1)[..., None]
    return vals.transpose(0, 1, 3, 2).reshape(g * 512, n)


K, T, E, C, N = 1536, 1024, 8, 128, 512


def by_expert(wq, xq):
    return np.concatenate([wq[e].T @ xq[:, e * C:(e + 1) * C] for e in range(E)], axis=1)


def setup_inputs():
    n = np.random.standard_normal
    s = mx_kscale(K)[:, None]
    packed = [pack_weight(m) for m in n((E, K, N)) / np.sqrt(K) / s[None]]
    return {
        "xT": (n((K, T)) * s).astype(np.float32),
        "w_words": np.stack([m[0] for m in packed]),
        "w_scales": np.stack([m[1] for m in packed]),
        "gate": np.tile(np.random.uniform(0.2, 1.0, E * C), (N, 1)).astype(np.float32),
        "offs": striped(np.random.permutation(T)[:E * C]),
    }


def reference(xT, w_words, w_scales, gate, offs):
    idx = unstriped(offs)
    xq = mxq(f64(xT)[:, idx], 0, "e4m3")
    w = np.stack([unpack_weight(w_words[e], w_scales[e]) for e in range(E)])
    y = by_expert(w, xq)
    out = np.zeros((N, T))
    out[:, idx] = f64(gate) * y
    return out

@@ -1,0 +1,137 @@
+from contextlib import ExitStack
+
+import concourse.mybir as mybir
+from concourse.masks import make_identity
+
+K, T, E, C, N = 1536, 1024, 8, 128, 512
+P = 128
+PACK = 4
+PASSES = K // (P * PACK)
+BLOCKS = N // P
+
+FLOPS = 2 * K * E * C * N
+BYTES = 4 * K * T + E * K * N + E * (K // 32) * N + 4 * E * C + 2 * P * (T // 16) + 4 * N * T
+
+F32 = mybir.dt.float32
+BF16 = mybir.dt.bfloat16
+I32 = mybir.dt.int32
+U32 = mybir.dt.uint32
+U16 = mybir.dt.uint16
+U8 = mybir.dt.uint8
+FP8X4 = mybir.dt.float8_e4m3fn_x4
+COPY = mybir.ActivationFunctionType.Copy
+
+CHUNKS = [
+    [(0, 512, "sv"), (512, 512, "sv")],
+    [(0, 512, "sv"), (512, 512, "ss")],
+    [(0, 512, "ss"), (512, 256, "v"), (768, 256, "s")],
+]
+PIECE = 256
+SLICE = 512
+GROUP = 2
+
+
+def tile_routed_moe_kernel(tc, xT, w_words, w_scales, gate, offs, out):
+    nc = tc.nc
+    with ExitStack() as ctx:
+        keep = ctx.enter_context(tc.tile_pool(name="keep", bufs=1))
+        ring = ctx.enter_context(tc.tile_pool(name="ring", bufs=3))
+        psum = ctx.enter_context(tc.psum_pool(name="psum", bufs=4))
+        psum_t = ctx.enter_context(tc.psum_pool(name="psum_t", bufs=3))
+        psum_g = ctx.enter_context(tc.psum_pool(name="psum_g", bufs=1))
+
+        planes_hbm = xT.rearrange("(g p t) n -> g p t n", p=P, t=PACK)
+        raws = {}
+        offs_sb = keep.tile([P, T // 16], U16, name="offs_sb")
+        gate_rows = keep.tile([P, P], F32, name="gate_rows")
+        nc.gpsimd.memset(gate_rows[:], 0.0)
+        first = True
+        for g in range(PASSES):
+            for t0, width, _ in CHUNKS[g]:
+                raw = keep.tile([P, PACK, width], F32, name=f"raw_{g}_{t0}")
+                nc.sync.dma_start(out=raw[:], in_=planes_hbm[g, :, :, t0 : t0 + width])
+                raws[g, t0] = raw
+                if first:
+                    nc.sync.dma_start(offs_sb[:], offs)
+                    first = False
+        wsc = keep.tile([P, E * PASSES, N], U8, name="wsc", align_bytes=64)
+        nc.vector.memset(wsc[:].rearrange("p c n -> p (c n)").bitcast(I32), 0)
+        flat = w_scales.rearrange("e a q n -> q (e a) n")
+        for q in range(4):
+            nc.sync.dma_start(
+                out=wsc[32 * q : 32 * q + 4, :, :].bitcast(I32), in_=flat[4 * q : 4 * q + 4, :, :].bitcast(I32)
+            )
+        nc.sync.dma_start(out=gate_rows[0:E, :], in_=gate[0:1, :].rearrange("o (e c) -> (o e) c", e=E))
+        wts = []
+        for e in range(E):
+            wt = keep.tile([P, PASSES, 4 * N], U8, name=f"wt_{e}", align_bytes=64)
+            nc.sync.dma_start(
+                out=wt[:].bitcast(I32), in_=w_words[e].rearrange("a p n r -> p a (n r)").bitcast(I32)
+            )
+            wts.append(wt)
+
+        ident = keep.tile([P, P], F32, name="ident")
+        make_identity(nc, ident[:])
+
+        codes = [keep.tile([P, T], U32, name=f"codes_{g}", align_bytes=64) for g in range(PASSES)]
+        scales = keep.tile([P, T], U8, name="scales", align_bytes=64)
+        g_codes = [keep.tile([P, T], U32, name=f"g_codes_{g}", align_bytes=64) for g in range(PASSES)]
+        g_scales = keep.tile([P, T], U8, name="g_scales", align_bytes=64)
+        nc.gpsimd.memset(scales[:], 0)
+
+        for g in range(PASSES):
+            for t0, width, engines in CHUNKS[g]:
+                grouped = keep.tile([P, width, PACK], BF16, name=f"grouped_{g}_{t0}", align_bytes=64)
+                for i, who in enumerate(engines):
+                    a, b = i * PIECE, (i + 1) * PIECE
+                    dst = grouped[:, a:b, :].rearrange("p (c i) t -> p c t i", i=4)
+                    src = raws[g, t0][:, :, a:b].rearrange("p t (c i) -> p c t i", i=4)
+                    if who == "s":
+                        nc.scalar.copy(dst, src)
+                    else:
+                        nc.vector.tensor_copy(dst, src)
+                for i in range(width // PIECE):
+                    a, b = i * PIECE, (i + 1) * PIECE
+                    nc.vector.quantize_mx(
+                        out=codes[g][:, t0 + a : t0 + b].bitcast(FP8X4),
+                        scales=scales[4 * g :, t0 + a : t0 + b],
+                        in_=grouped[:, a:b, :].rearrange("p w t -> p (w t)"),
+                    )
+            for s0 in range(0, T, SLICE):
+                picks = offs_sb[:, s0 // 16 : (s0 + SLICE) // 16]
+                nc.vector.tensor_copy(g_codes[g][:, s0 : s0 + SLICE], codes[g][:].indirect(picks))
+                if g == PASSES - 1:
+                    nc.vector.tensor_copy(g_scales[:, s0 : s0 + SLICE], scales[:].indirect(picks))
+
+        gate_ps = psum_g.tile([P, P], F32, name="gate_ps")
+        nc.tensor.transpose(gate_ps[:], gate_rows[:], ident[:])
+        gate_cols = keep.tile([P, E], F32, name="gate_cols")
+        nc.scalar.copy(gate_cols[:], gate_ps[:, 0:E])
+
+        windows = [keep.tile([P, T], F32, name=f"window_{b}") for b in range(BLOCKS)]
+        for e0 in range(0, E, GROUP):
+            yT = keep.tile([P, BLOCKS, GROUP * C], F32, name=f"yT_{e0}")
+            for e in range(e0, e0 + GROUP):
+                slots = slice(e * C, (e + 1) * C)
+                acc = psum.tile([P, N], F32, name="acc")
+                for a in range(PASSES):
+                    nc.tensor.matmul_mx(
+                        out=acc[:],
+                        lhsT=g_codes[a][:, slots].bitcast(FP8X4),
+                        lhsT_scale=g_scales[4 * a :, slots],
+                        rhs=wts[e][:, a, :].bitcast(FP8X4),
+                        rhs_scale=wsc[:, e * PASSES + a, :],
+                        start=(a == 0),
+                        stop=(a == PASSES - 1),
+                    )
+                y = ring.tile([P, N], F32, name="y")
+                nc.scalar.activation(y[:], acc[:], COPY, scale=gate_cols[:, e : e + 1])
+                turned = psum_t.tile([P, BLOCKS, P], F32, name="turned")
+                for b in range(BLOCKS):
+                    nc.tensor.transpose(turned[:, b, :], y[:, b * P : (b + 1) * P], ident[:])
+                nc.scalar.copy(yT[:, :, (e - e0) * C : (e - e0 + 1) * C], turned[:])
+            picks = offs_sb[:, e0 * C // 16 : (e0 + GROUP) * C // 16]
+            for b in range(BLOCKS):
+                nc.vector.tensor_copy(windows[b][:].indirect(picks), yT[:, b, :])
+        for b in range(BLOCKS):
+            nc.sync.dma_start(out=out[b * P : (b + 1) * P, :], in_=windows[b][:])

@@ -1,7 +1,6 @@
 from contextlib import ExitStack
 
 import concourse.mybir as mybir
-from concourse.masks import make_identity
 
 K, T, E, C, N = 1536, 1024, 8, 128, 512
 P = 128
@@ -19,119 +18,114 @@ U32 = mybir.dt.uint32
 U16 = mybir.dt.uint16
 U8 = mybir.dt.uint8
 FP8X4 = mybir.dt.float8_e4m3fn_x4
-COPY = mybir.ActivationFunctionType.Copy
+MULT = mybir.AluOpType.mult
 
 CHUNKS = [
-    [(0, 512, "sv"), (512, 512, "sv")],
-    [(0, 512, "sv"), (512, 512, "ss")],
-    [(0, 512, "ss"), (512, 256, "v"), (768, 256, "s")],
+    [(0, 512, [(256, "v"), (256, "s")]), (512, 512, [(256, "v"), (256, "s")])],
+    [(0, 512, [(256, "s"), (256, "s")]), (512, 512, [(256, "v"), (256, "s")])],
+    [(0, 512, [(256, "s"), (256, "s")]), (512, 512, [(256, "v"), (128, "v"), (128, "s")])],
 ]
-PIECE = 256
-SLICE = 512
-GROUP = 2
+QUANT = 256
+SLICES = [[(0, 512), (512, 512)], [(0, 512), (512, 512)], [(0, 512), (512, 512)]]
+GROUPS = [(0, 2), (2, 2), (4, 4)]
+SCALE_GROUPS = [(0, 2), (2, 6)]
 
 
 def tile_routed_moe_kernel(tc, xT, w_words, w_scales, gate, offs, out):
     nc = tc.nc
     with ExitStack() as ctx:
         keep = ctx.enter_context(tc.tile_pool(name="keep", bufs=1))
-        ring = ctx.enter_context(tc.tile_pool(name="ring", bufs=3))
-        psum = ctx.enter_context(tc.psum_pool(name="psum", bufs=4))
-        psum_t = ctx.enter_context(tc.psum_pool(name="psum_t", bufs=3))
-        psum_g = ctx.enter_context(tc.psum_pool(name="psum_g", bufs=1))
+        psum = ctx.enter_context(tc.psum_pool(name="psum", bufs=8))
 
         planes_hbm = xT.rearrange("(g p t) n -> g p t n", p=P, t=PACK)
         raws = {}
         offs_sb = keep.tile([P, T // 16], U16, name="offs_sb")
-        gate_rows = keep.tile([P, P], F32, name="gate_rows")
-        nc.gpsimd.memset(gate_rows[:], 0.0)
-        first = True
         for g in range(PASSES):
-            for t0, width, _ in CHUNKS[g]:
+            for t0, width, pieces in CHUNKS[g]:
                 raw = keep.tile([P, PACK, width], F32, name=f"raw_{g}_{t0}")
                 nc.sync.dma_start(out=raw[:], in_=planes_hbm[g, :, :, t0 : t0 + width])
                 raws[g, t0] = raw
-                if first:
+                if g == 0 and t0 == 0:
                     nc.sync.dma_start(offs_sb[:], offs)
-                    first = False
-        wsc = keep.tile([P, E * PASSES, N], U8, name="wsc", align_bytes=64)
-        nc.vector.memset(wsc[:].rearrange("p c n -> p (c n)").bitcast(I32), 0)
         flat = w_scales.rearrange("e a q n -> q (e a) n")
-        for q in range(4):
-            nc.sync.dma_start(
-                out=wsc[32 * q : 32 * q + 4, :, :].bitcast(I32), in_=flat[4 * q : 4 * q + 4, :, :].bitcast(I32)
-            )
-        nc.sync.dma_start(out=gate_rows[0:E, :], in_=gate[0:1, :].rearrange("o (e c) -> (o e) c", e=E))
+        wsc = {}
         wts = []
+        gate_sb = keep.tile([P, E * C], F32, name="gate_sb")
         for e in range(E):
+            for e0, count in SCALE_GROUPS:
+                if e == e0:
+                    sc = keep.tile([P, count * PASSES, N], U8, name=f"wsc_{e0}", align_bytes=64)
+                    nc.vector.memset(sc[:].rearrange("p c n -> p (c n)").bitcast(I32), 0)
+                    for q in range(4):
+                        nc.sync.dma_start(
+                            out=sc[32 * q : 32 * q + 4, :, :].bitcast(I32),
+                            in_=flat[4 * q : 4 * q + 4, e0 * PASSES : (e0 + count) * PASSES, :].bitcast(I32),
+                        )
+                    for i in range(count):
+                        wsc[e0 + i] = sc[:, i * PASSES : (i + 1) * PASSES, :]
             wt = keep.tile([P, PASSES, 4 * N], U8, name=f"wt_{e}", align_bytes=64)
             nc.sync.dma_start(
                 out=wt[:].bitcast(I32), in_=w_words[e].rearrange("a p n r -> p a (n r)").bitcast(I32)
             )
             wts.append(wt)
-
-        ident = keep.tile([P, P], F32, name="ident")
-        make_identity(nc, ident[:])
+            if e == 1:
+                nc.sync.dma_start(out=gate_sb[:], in_=gate[0:P, :])
 
         codes = [keep.tile([P, T], U32, name=f"codes_{g}", align_bytes=64) for g in range(PASSES)]
-        scales = keep.tile([P, T], U8, name="scales", align_bytes=64)
         g_codes = [keep.tile([P, T], U32, name=f"g_codes_{g}", align_bytes=64) for g in range(PASSES)]
+        scales = keep.tile([P, T], U8, name="scales", align_bytes=64)
         g_scales = keep.tile([P, T], U8, name="g_scales", align_bytes=64)
         nc.gpsimd.memset(scales[:], 0)
 
         for g in range(PASSES):
-            for t0, width, engines in CHUNKS[g]:
+            for t0, width, pieces in CHUNKS[g]:
                 grouped = keep.tile([P, width, PACK], BF16, name=f"grouped_{g}_{t0}", align_bytes=64)
-                for i, who in enumerate(engines):
-                    a, b = i * PIECE, (i + 1) * PIECE
+                a = 0
+                for size, who in pieces:
+                    b = a + size
                     dst = grouped[:, a:b, :].rearrange("p (c i) t -> p c t i", i=4)
                     src = raws[g, t0][:, :, a:b].rearrange("p t (c i) -> p c t i", i=4)
                     if who == "s":
                         nc.scalar.copy(dst, src)
                     else:
                         nc.vector.tensor_copy(dst, src)
-                for i in range(width // PIECE):
-                    a, b = i * PIECE, (i + 1) * PIECE
+                    a = b
+                step = min(QUANT, width)
+                for a in range(0, width, step):
+                    b = a + step
                     nc.vector.quantize_mx(
                         out=codes[g][:, t0 + a : t0 + b].bitcast(FP8X4),
                         scales=scales[4 * g :, t0 + a : t0 + b],
                         in_=grouped[:, a:b, :].rearrange("p w t -> p (w t)"),
                     )
-            for s0 in range(0, T, SLICE):
-                picks = offs_sb[:, s0 // 16 : (s0 + SLICE) // 16]
-                nc.vector.tensor_copy(g_codes[g][:, s0 : s0 + SLICE], codes[g][:].indirect(picks))
+            for s0, n in SLICES[g]:
+                picks = offs_sb[:, s0 // 16 : (s0 + n) // 16]
+                nc.vector.tensor_copy(g_codes[g][:, s0 : s0 + n], codes[g][:].indirect(picks))
                 if g == PASSES - 1:
-                    nc.vector.tensor_copy(g_scales[:, s0 : s0 + SLICE], scales[:].indirect(picks))
-
-        gate_ps = psum_g.tile([P, P], F32, name="gate_ps")
-        nc.tensor.transpose(gate_ps[:], gate_rows[:], ident[:])
-        gate_cols = keep.tile([P, E], F32, name="gate_cols")
-        nc.scalar.copy(gate_cols[:], gate_ps[:, 0:E])
+                    nc.vector.tensor_copy(g_scales[:, s0 : s0 + n], scales[:].indirect(picks))
 
         windows = [keep.tile([P, T], F32, name=f"window_{b}") for b in range(BLOCKS)]
-        for e0 in range(0, E, GROUP):
-            yT = keep.tile([P, BLOCKS, GROUP * C], F32, name=f"yT_{e0}")
-            for e in range(e0, e0 + GROUP):
-                slots = slice(e * C, (e + 1) * C)
-                acc = psum.tile([P, N], F32, name="acc")
-                for a in range(PASSES):
-                    nc.tensor.matmul_mx(
-                        out=acc[:],
-                        lhsT=g_codes[a][:, slots].bitcast(FP8X4),
-                        lhsT_scale=g_scales[4 * a :, slots],
-                        rhs=wts[e][:, a, :].bitcast(FP8X4),
-                        rhs_scale=wsc[:, e * PASSES + a, :],
-                        start=(a == 0),
-                        stop=(a == PASSES - 1),
-                    )
-                y = ring.tile([P, N], F32, name="y")
-                nc.scalar.activation(y[:], acc[:], COPY, scale=gate_cols[:, e : e + 1])
-                turned = psum_t.tile([P, BLOCKS, P], F32, name="turned")
-                for b in range(BLOCKS):
-                    nc.tensor.transpose(turned[:, b, :], y[:, b * P : (b + 1) * P], ident[:])
-                nc.scalar.copy(yT[:, :, (e - e0) * C : (e - e0 + 1) * C], turned[:])
-            picks = offs_sb[:, e0 * C // 16 : (e0 + GROUP) * C // 16]
+        for e0, count in GROUPS:
+            y = keep.tile([P, BLOCKS, count * C], F32, name=f"y_{e0}")
+            slots = slice(e0 * C, (e0 + count) * C)
             for b in range(BLOCKS):
-                nc.vector.tensor_copy(windows[b][:].indirect(picks), yT[:, b, :])
+                features = slice(b * P, (b + 1) * P)
+                acc = psum.tile([P, count * C], F32, name="acc")
+                for i in range(count):
+                    own = slice((e0 + i) * C, (e0 + i + 1) * C)
+                    for a in range(PASSES):
+                        nc.tensor.matmul_mx(
+                            out=acc[:, i * C : (i + 1) * C],
+                            lhsT=wts[e0 + i][:, a, 4 * b * P : 4 * (b + 1) * P].bitcast(FP8X4),
+                            lhsT_scale=wsc[e0 + i][:, a, features],
+                            rhs=g_codes[a][:, own].bitcast(FP8X4),
+                            rhs_scale=g_scales[4 * a :, own],
+                            start=(a == 0),
+                            stop=(a == PASSES - 1),
+                        )
+                nc.scalar.copy(y[:, b, :], acc[:])
+            picks = offs_sb[:, e0 * C // 16 : (e0 + count) * C // 16]
+            for b in range(BLOCKS):
+                nc.vector.tensor_tensor(windows[b][:].indirect(picks), y[:, b, :], gate_sb[:, slots], MULT)
         for b in range(BLOCKS):
             nc.sync.dma_start(out=out[b * P : (b + 1) * P, :], in_=windows[b][:])

@@ -21,14 +21,14 @@ FP8X4 = mybir.dt.float8_e4m3fn_x4
 MULT = mybir.AluOpType.mult
 
 CHUNKS = [
-    [(0, 512, [(256, "v"), (256, "s")]), (512, 512, [(256, "v"), (256, "s")])],
-    [(0, 512, [(256, "s"), (256, "s")]), (512, 512, [(256, "v"), (256, "s")])],
-    [(0, 512, [(256, "s"), (256, "s")]), (512, 512, [(256, "v"), (128, "v"), (128, "s")])],
+    [(0, 1024, [(512, "v"), (512, "s")])],
+    [(0, 1024, [(512, "v"), (512, "s")])],
+    [(0, 512, [(256, "s"), (256, "s")]), (512, 512, [(256, "s"), (256, "s")])],
 ]
-QUANT = 256
+QUANT = 512
 SLICES = [[(0, 512), (512, 512)], [(0, 512), (512, 512)], [(0, 512), (512, 512)]]
-GROUPS = [(0, 2), (2, 2), (4, 4)]
-SCALE_GROUPS = [(0, 2), (2, 6)]
+GROUPS = [(0, 2), (2, 2), (4, 2), (6, 2)]
+SCALE_GROUPS = [(0, 2), (2, 3), (5, 3)]
 
 
 def tile_routed_moe_kernel(tc, xT, w_words, w_scales, gate, offs, out):

@@ -21,13 +21,13 @@ FP8X4 = mybir.dt.float8_e4m3fn_x4
 MULT = mybir.AluOpType.mult
 
 CHUNKS = [
-    [(0, 1024, [(512, "v"), (512, "s")])],
-    [(0, 1024, [(512, "v"), (512, "s")])],
-    [(0, 512, [(256, "s"), (256, "s")]), (512, 512, [(256, "s"), (256, "s")])],
+    [(0, 1024, [(640, "v"), (384, "s")])],
+    [(0, 512, [(512, "s")]), (512, 512, [(128, "v"), (384, "s")])],
+    [(0, 512, [(512, "s")]), (512, 512, [(256, "v"), (256, "s")])],
 ]
 QUANT = 512
 SLICES = [[(0, 512), (512, 512)], [(0, 512), (512, 512)], [(0, 512), (512, 512)]]
-GROUPS = [(0, 2), (2, 2), (4, 2), (6, 2)]
+GROUPS = [(0, 2), (2, 3), (5, 3)]
 SCALE_GROUPS = [(0, 2), (2, 3), (5, 3)]
 
 
@@ -50,7 +50,7 @@ def tile_routed_moe_kernel(tc, xT, w_words, w_scales, gate, offs, out):
         flat = w_scales.rearrange("e a q n -> q (e a) n")
         wsc = {}
         wts = []
-        gate_sb = keep.tile([P, E * C], F32, name="gate_sb")
+        gates = {}
         for e in range(E):
             for e0, count in SCALE_GROUPS:
                 if e == e0:
@@ -68,8 +68,10 @@ def tile_routed_moe_kernel(tc, xT, w_words, w_scales, gate, offs, out):
                 out=wt[:].bitcast(I32), in_=w_words[e].rearrange("a p n r -> p a (n r)").bitcast(I32)
             )
             wts.append(wt)
-            if e == 1:
-                nc.sync.dma_start(out=gate_sb[:], in_=gate[0:P, :])
+            for e0, count in GROUPS:
+                if e == e0 + 0:
+                    gates[e0] = keep.tile([P, count * C], F32, name=f"gate_{e0}")
+                    nc.sync.dma_start(out=gates[e0][:], in_=gate[0:P, e0 * C : (e0 + count) * C])
 
         codes = [keep.tile([P, T], U32, name=f"codes_{g}", align_bytes=64) for g in range(PASSES)]
         g_codes = [keep.tile([P, T], U32, name=f"g_codes_{g}", align_bytes=64) for g in range(PASSES)]
@@ -77,6 +79,7 @@ def tile_routed_moe_kernel(tc, xT, w_words, w_scales, gate, offs, out):
         g_scales = keep.tile([P, T], U8, name="g_scales", align_bytes=64)
         nc.gpsimd.memset(scales[:], 0)
 
+        grouped_of = {}
         for g in range(PASSES):
             for t0, width, pieces in CHUNKS[g]:
                 grouped = keep.tile([P, width, PACK], BF16, name=f"grouped_{g}_{t0}", align_bytes=64)
@@ -90,6 +93,9 @@ def tile_routed_moe_kernel(tc, xT, w_words, w_scales, gate, offs, out):
                     else:
                         nc.vector.tensor_copy(dst, src)
                     a = b
+                grouped_of[g, t0] = grouped
+            for t0, width, pieces in CHUNKS[g]:
+                grouped = grouped_of[g, t0]
                 step = min(QUANT, width)
                 for a in range(0, width, step):
                     b = a + step
@@ -107,7 +113,6 @@ def tile_routed_moe_kernel(tc, xT, w_words, w_scales, gate, offs, out):
         windows = [keep.tile([P, T], F32, name=f"window_{b}") for b in range(BLOCKS)]
         for e0, count in GROUPS:
             y = keep.tile([P, BLOCKS, count * C], F32, name=f"y_{e0}")
-            slots = slice(e0 * C, (e0 + count) * C)
             for b in range(BLOCKS):
                 features = slice(b * P, (b + 1) * P)
                 acc = psum.tile([P, count * C], F32, name="acc")
@@ -126,6 +131,6 @@ def tile_routed_moe_kernel(tc, xT, w_words, w_scales, gate, offs, out):
                 nc.scalar.copy(y[:, b, :], acc[:])
             picks = offs_sb[:, e0 * C // 16 : (e0 + count) * C // 16]
             for b in range(BLOCKS):
-                nc.vector.tensor_tensor(windows[b][:].indirect(picks), y[:, b, :], gate_sb[:, slots], MULT)
+                nc.vector.tensor_tensor(windows[b][:].indirect(picks), y[:, b, :], gates[e0][:], MULT)
         for b in range(BLOCKS):
             nc.sync.dma_start(out=out[b * P : (b + 1) * P, :], in_=windows[b][:])

@@ -21,13 +21,13 @@ FP8X4 = mybir.dt.float8_e4m3fn_x4
 MULT = mybir.AluOpType.mult
 
 CHUNKS = [
-    [(0, 1024, [(640, "v"), (384, "s")])],
-    [(0, 512, [(512, "s")]), (512, 512, [(128, "v"), (384, "s")])],
-    [(0, 512, [(512, "s")]), (512, 512, [(256, "v"), (256, "s")])],
+    [(0, 512, [(256, "v"), (256, "s")]), (512, 512, [(256, "v"), (256, "s")])],
+    [(0, 1024, [(512, "s"), (512, "v")])],
+    [(0, 512, [(128, "v"), (384, "s")]), (512, 256, [(256, "s")]), (768, 256, [(256, "s")])],
 ]
-QUANT = 512
+QUANT = [256, 512, 512]
 SLICES = [[(0, 512), (512, 512)], [(0, 512), (512, 512)], [(0, 512), (512, 512)]]
-GROUPS = [(0, 2), (2, 3), (5, 3)]
+GROUPS = [(0, 2), (2, 2), (4, 2), (6, 2)]
 SCALE_GROUPS = [(0, 2), (2, 3), (5, 3)]
 
 
@@ -69,7 +69,7 @@ def tile_routed_moe_kernel(tc, xT, w_words, w_scales, gate, offs, out):
             )
             wts.append(wt)
             for e0, count in GROUPS:
-                if e == e0 + 0:
+                if e == e0 + count - 1:
                     gates[e0] = keep.tile([P, count * C], F32, name=f"gate_{e0}")
                     nc.sync.dma_start(out=gates[e0][:], in_=gate[0:P, e0 * C : (e0 + count) * C])
 
@@ -96,7 +96,7 @@ def tile_routed_moe_kernel(tc, xT, w_words, w_scales, gate, offs, out):
                 grouped_of[g, t0] = grouped
             for t0, width, pieces in CHUNKS[g]:
                 grouped = grouped_of[g, t0]
-                step = min(QUANT, width)
+                step = min(QUANT[g], width)
                 for a in range(0, width, step):
                     b = a + step
                     nc.vector.quantize_mx(

from contextlib import ExitStack

import concourse.mybir as mybir

K, T, E, C, N = 1536, 1024, 8, 128, 512
P = 128
PACK = 4
PASSES = K // (P * PACK)
BLOCKS = N // P

FLOPS = 2 * K * E * C * N
BYTES = 4 * K * T + E * K * N + E * (K // 32) * N + 4 * E * C + 2 * P * (T // 16) + 4 * N * T

F32 = mybir.dt.float32
BF16 = mybir.dt.bfloat16
I32 = mybir.dt.int32
U32 = mybir.dt.uint32
U16 = mybir.dt.uint16
U8 = mybir.dt.uint8
FP8X4 = mybir.dt.float8_e4m3fn_x4
MULT = mybir.AluOpType.mult

CHUNKS = [
    [(0, 512, [(256, "v"), (256, "s")]), (512, 512, [(256, "v"), (256, "s")])],
    [(0, 1024, [(512, "s"), (512, "v")])],
    [(0, 512, [(128, "v"), (384, "s")]), (512, 256, [(256, "s")]), (768, 256, [(256, "s")])],
]
QUANT = [256, 512, 512]
SLICES = [[(0, 512), (512, 512)], [(0, 512), (512, 512)], [(0, 512), (512, 512)]]
GROUPS = [(0, 2), (2, 2), (4, 2), (6, 2)]
SCALE_GROUPS = [(0, 2), (2, 3), (5, 3)]


def tile_routed_moe_kernel(tc, xT, w_words, w_scales, gate, offs, out):
    nc = tc.nc
    with ExitStack() as ctx:
        keep = ctx.enter_context(tc.tile_pool(name="keep", bufs=1))
        psum = ctx.enter_context(tc.psum_pool(name="psum", bufs=8))

        planes_hbm = xT.rearrange("(g p t) n -> g p t n", p=P, t=PACK)
        raws = {}
        offs_sb = keep.tile([P, T // 16], U16, name="offs_sb")
        for g in range(PASSES):
            for t0, width, pieces in CHUNKS[g]:
                raw = keep.tile([P, PACK, width], F32, name=f"raw_{g}_{t0}")
                nc.sync.dma_start(out=raw[:], in_=planes_hbm[g, :, :, t0 : t0 + width])
                raws[g, t0] = raw
                if g == 0 and t0 == 0:
                    nc.sync.dma_start(offs_sb[:], offs)
        flat = w_scales.rearrange("e a q n -> q (e a) n")
        wsc = {}
        wts = []
        gates = {}
        for e in range(E):
            for e0, count in SCALE_GROUPS:
                if e == e0:
                    sc = keep.tile([P, count * PASSES, N], U8, name=f"wsc_{e0}", align_bytes=64)
                    nc.vector.memset(sc[:].rearrange("p c n -> p (c n)").bitcast(I32), 0)
                    for q in range(4):
                        nc.sync.dma_start(
                            out=sc[32 * q : 32 * q + 4, :, :].bitcast(I32),
                            in_=flat[4 * q : 4 * q + 4, e0 * PASSES : (e0 + count) * PASSES, :].bitcast(I32),
                        )
                    for i in range(count):
                        wsc[e0 + i] = sc[:, i * PASSES : (i + 1) * PASSES, :]
            wt = keep.tile([P, PASSES, 4 * N], U8, name=f"wt_{e}", align_bytes=64)
            nc.sync.dma_start(
                out=wt[:].bitcast(I32), in_=w_words[e].rearrange("a p n r -> p a (n r)").bitcast(I32)
            )
            wts.append(wt)
            for e0, count in GROUPS:
                if e == e0 + count - 1:
                    gates[e0] = keep.tile([P, count * C], F32, name=f"gate_{e0}")
                    nc.sync.dma_start(out=gates[e0][:], in_=gate[0:P, e0 * C : (e0 + count) * C])

        codes = [keep.tile([P, T], U32, name=f"codes_{g}", align_bytes=64) for g in range(PASSES)]
        g_codes = [keep.tile([P, T], U32, name=f"g_codes_{g}", align_bytes=64) for g in range(PASSES)]
        scales = keep.tile([P, T], U8, name="scales", align_bytes=64)
        g_scales = keep.tile([P, T], U8, name="g_scales", align_bytes=64)
        nc.gpsimd.memset(scales[:], 0)

        grouped_of = {}
        for g in range(PASSES):
            for t0, width, pieces in CHUNKS[g]:
                grouped = keep.tile([P, width, PACK], BF16, name=f"grouped_{g}_{t0}", align_bytes=64)
                a = 0
                for size, who in pieces:
                    b = a + size
                    dst = grouped[:, a:b, :].rearrange("p (c i) t -> p c t i", i=4)
                    src = raws[g, t0][:, :, a:b].rearrange("p t (c i) -> p c t i", i=4)
                    if who == "s":
                        nc.scalar.copy(dst, src)
                    else:
                        nc.vector.tensor_copy(dst, src)
                    a = b
                grouped_of[g, t0] = grouped
            for t0, width, pieces in CHUNKS[g]:
                grouped = grouped_of[g, t0]
                step = min(QUANT[g], width)
                for a in range(0, width, step):
                    b = a + step
                    nc.vector.quantize_mx(
                        out=codes[g][:, t0 + a : t0 + b].bitcast(FP8X4),
                        scales=scales[4 * g :, t0 + a : t0 + b],
                        in_=grouped[:, a:b, :].rearrange("p w t -> p (w t)"),
                    )
            for s0, n in SLICES[g]:
                picks = offs_sb[:, s0 // 16 : (s0 + n) // 16]
                nc.vector.tensor_copy(g_codes[g][:, s0 : s0 + n], codes[g][:].indirect(picks))
                if g == PASSES - 1:
                    nc.vector.tensor_copy(g_scales[:, s0 : s0 + n], scales[:].indirect(picks))

        windows = [keep.tile([P, T], F32, name=f"window_{b}") for b in range(BLOCKS)]
        for e0, count in GROUPS:
            y = keep.tile([P, BLOCKS, count * C], F32, name=f"y_{e0}")
            for b in range(BLOCKS):
                features = slice(b * P, (b + 1) * P)
                acc = psum.tile([P, count * C], F32, name="acc")
                for i in range(count):
                    own = slice((e0 + i) * C, (e0 + i + 1) * C)
                    for a in range(PASSES):
                        nc.tensor.matmul_mx(
                            out=acc[:, i * C : (i + 1) * C],
                            lhsT=wts[e0 + i][:, a, 4 * b * P : 4 * (b + 1) * P].bitcast(FP8X4),
                            lhsT_scale=wsc[e0 + i][:, a, features],
                            rhs=g_codes[a][:, own].bitcast(FP8X4),
                            rhs_scale=g_scales[4 * a :, own],
                            start=(a == 0),
                            stop=(a == PASSES - 1),
                        )
                nc.scalar.copy(y[:, b, :], acc[:])
            picks = offs_sb[:, e0 * C // 16 : (e0 + count) * C // 16]
            for b in range(BLOCKS):
                nc.vector.tensor_tensor(windows[b][:].indirect(picks), y[:, b, :], gates[e0][:], MULT)
        for b in range(BLOCKS):
            nc.sync.dma_start(out=out[b * P : (b + 1) * P, :], in_=windows[b][:])
